import numpy as np
import ml_dtypes

BF16 = ml_dtypes.bfloat16


def bf(x):
    return np.asarray(x, np.float32).astype(BF16)


def f32(x):
    return np.asarray(x, np.float32)


def f64(x):
    return np.asarray(x).astype(np.float64)


def striped(idx):
    return np.tile(idx.reshape(-1, 16).T, (8, 1))


S, K, M, N, E, Q = 2048, 256, 128, 4096, 4, 1024


def two_experts():
    first = np.random.permutation(S).reshape(E, S // E)
    return np.concatenate([np.random.permutation(np.concatenate([first[e], first[(e + 1) % E]])) for e in range(E)])


def setup_inputs():
    return {"table": bf(np.random.standard_normal((K, S))), "w": bf(np.random.standard_normal((E, K, M)) / np.sqrt(K)), "b": f32(0.5 * np.random.standard_normal((M, 1))), "offs": striped(two_experts())}


def reference(table, w, b, offs):
    idx = offs[:16].T.reshape(-1)
    x = f64(table)[:, idx]
    y = np.concatenate([f64(w)[e].T @ x[:, e * Q : (e + 1) * Q] for e in range(E)], axis=1)
    return np.maximum(y + f64(b), 0.0)

@@ -1,0 +1,53 @@
+import concourse.mybir as mybir
+
+BF16, F32, U16 = mybir.dt.bfloat16, mybir.dt.float32, mybir.dt.uint16
+ADD, MAX = mybir.AluOpType.add, mybir.AluOpType.max
+RELU = mybir.ActivationFunctionType.Relu
+
+P = 128
+TOKENS, K, M, N, EXPERTS = 2048, 256, 128, 4096, 4
+BLOCKS = K // P
+COLS = 512
+TILES = N // COLS
+TILES_PER_EXPERT = TILES // EXPERTS
+LIST_COLS = COLS // 16
+
+FLOPS = 2 * N * K * M
+
+
+def tile_gather_matmul_kernel(tc, table, w, b, offs, out):
+    nc = tc.nc
+    with (
+        tc.tile_pool(name="held", bufs=1) as held,
+        tc.tile_pool(name="results", bufs=TILES) as results,
+        tc.psum_pool(name="psum", bufs=TILES) as psum,
+    ):
+        offsets = held.tile([P, N // 16], U16)
+        weights = held.tile([P, EXPERTS, BLOCKS, M], BF16)
+        bias = held.tile([P, 1], F32)
+        features = [held.tile([P, TOKENS], BF16, name=f"features{a}") for a in range(BLOCKS)]
+
+        nc.sync.dma_start(offsets[:], offs)
+        for a in range(BLOCKS):
+            nc.sync.dma_start(features[a][:], table[a * P : (a + 1) * P, :])
+        nc.scalar.dma_start(weights[:], w.rearrange("e (a p) m -> p e a m", p=P))
+        nc.scalar.dma_start(bias[:], b)
+
+        for t in range(TILES):
+            expert = t // TILES_PER_EXPERT
+            picked = offsets[:, t * LIST_COLS : (t + 1) * LIST_COLS]
+            sums = psum.tile([P, COLS], F32)
+            for a in range(BLOCKS):
+                nc.tensor.matmul(
+                    sums[:],
+                    weights[:, expert, a, :],
+                    features[a][:].indirect(picked),
+                    start=(a == 0),
+                    stop=(a == BLOCKS - 1),
+                )
+            result = results.tile([P, COLS], F32)
+            if t % 2 == 0:
+                nc.vector.tensor_scalar(result[:], sums[:], bias[:], 0.0, ADD, MAX)
+            else:
+                nc.scalar.activation(result[:], sums[:], RELU, bias=bias[:])
+            nc.sync.dma_start(out[:, t * COLS : (t + 1) * COLS], result[:])

@@ -20,34 +20,49 @@ def tile_gather_matmul_kernel(tc, table, w, b, offs, out):
     with (
         tc.tile_pool(name="held", bufs=1) as held,
         tc.tile_pool(name="results", bufs=TILES) as results,
-        tc.psum_pool(name="psum", bufs=TILES) as psum,
+        tc.psum_pool(name="psum", bufs=1) as psum,
     ):
         offsets = held.tile([P, N // 16], U16)
-        weights = held.tile([P, EXPERTS, BLOCKS, M], BF16)
         bias = held.tile([P, 1], F32)
         features = [held.tile([P, TOKENS], BF16, name=f"features{a}") for a in range(BLOCKS)]
+        weights = [held.tile([P, EXPERTS // 2, BLOCKS, M], BF16, name=f"weights{h}") for h in range(2)]
+
+        table_blocks = table.rearrange("(p a) s -> a p s", a=BLOCKS)
+        w_blocks = w.rearrange("e (p a) m -> p e a m", a=BLOCKS)
 
         nc.sync.dma_start(offsets[:], offs)
-        for a in range(BLOCKS):
-            nc.sync.dma_start(features[a][:], table[a * P : (a + 1) * P, :])
-        nc.scalar.dma_start(weights[:], w.rearrange("e (a p) m -> p e a m", p=P))
+        nc.sync.dma_start(features[0][:], table_blocks[0])
+        nc.scalar.dma_start(weights[0][:], w_blocks[:, : EXPERTS // 2])
+        nc.sync.dma_start(features[1][:], table_blocks[1])
+        nc.sync.dma_start(weights[1][:], w_blocks[:, EXPERTS // 2 :])
         nc.scalar.dma_start(bias[:], b)
 
-        for t in range(TILES):
+        sums = [psum.tile([P, COLS], F32, name=f"sums{t}") for t in range(TILES)]
+
+        def multiply(t, a):
             expert = t // TILES_PER_EXPERT
-            picked = offsets[:, t * LIST_COLS : (t + 1) * LIST_COLS]
-            sums = psum.tile([P, COLS], F32)
-            for a in range(BLOCKS):
-                nc.tensor.matmul(
-                    sums[:],
-                    weights[:, expert, a, :],
-                    features[a][:].indirect(picked),
-                    start=(a == 0),
-                    stop=(a == BLOCKS - 1),
-                )
+            nc.tensor.matmul(
+                sums[t][:],
+                weights[expert // 2][:, expert % 2, a, :],
+                features[a][:].indirect(offsets[:, t * LIST_COLS : (t + 1) * LIST_COLS]),
+                start=(a == 0),
+                stop=(a == BLOCKS - 1),
+            )
+
+        def finish(t):
             result = results.tile([P, COLS], F32)
-            if t % 2 == 0:
-                nc.vector.tensor_scalar(result[:], sums[:], bias[:], 0.0, ADD, MAX)
+            if t % 2 == 1:
+                nc.vector.tensor_scalar(result[:], sums[t][:], bias[:], 0.0, ADD, MAX)
             else:
-                nc.scalar.activation(result[:], sums[:], RELU, bias=bias[:])
+                nc.scalar.activation(result[:], sums[t][:], RELU, bias=bias[:])
             nc.sync.dma_start(out[:, t * COLS : (t + 1) * COLS], result[:])
+
+        for t in range(TILES // 2):
+            multiply(t, 0)
+        for t in range(TILES // 2):
+            multiply(t, 1)
+            finish(t)
+        for t in range(TILES // 2, TILES):
+            for a in range(BLOCKS):
+                multiply(t, a)
+            finish(t)

@@ -19,7 +19,7 @@ def tile_gather_matmul_kernel(tc, table, w, b, offs, out):
     nc = tc.nc
     with (
         tc.tile_pool(name="held", bufs=1) as held,
-        tc.tile_pool(name="results", bufs=TILES) as results,
+        tc.tile_pool(name="results", bufs=1) as results,
         tc.psum_pool(name="psum", bufs=1) as psum,
     ):
         offsets = held.tile([P, N // 16], U16)
@@ -50,12 +50,17 @@ def tile_gather_matmul_kernel(tc, table, w, b, offs, out):
             )
 
         def finish(t):
-            result = results.tile([P, COLS], F32)
-            if t % 2 == 1:
-                nc.vector.tensor_scalar(result[:], sums[t][:], bias[:], 0.0, ADD, MAX)
-            else:
-                nc.scalar.activation(result[:], sums[t][:], RELU, bias=bias[:])
-            nc.sync.dma_start(out[:, t * COLS : (t + 1) * COLS], result[:])
+            parts = 2 if t == TILES - 1 else 1
+            width = COLS // parts
+            for h in range(parts):
+                result = results.tile([P, width], F32, name=f"result{t}_{h}")
+                source = sums[t][:, h * width : (h + 1) * width]
+                if t % 2 == 1:
+                    nc.vector.tensor_scalar(result[:], source, bias[:], 0.0, ADD, MAX)
+                else:
+                    nc.scalar.activation(result[:], source, RELU, bias=bias[:])
+                first = t * COLS + h * width
+                nc.sync.dma_start(out[:, first : first + width], result[:])
 
         for t in range(TILES // 2):
             multiply(t, 0)

import concourse.mybir as mybir

BF16, F32, U16 = mybir.dt.bfloat16, mybir.dt.float32, mybir.dt.uint16
ADD, MAX = mybir.AluOpType.add, mybir.AluOpType.max
RELU = mybir.ActivationFunctionType.Relu

P = 128
TOKENS, K, M, N, EXPERTS = 2048, 256, 128, 4096, 4
BLOCKS = K // P
COLS = 512
TILES = N // COLS
TILES_PER_EXPERT = TILES // EXPERTS
LIST_COLS = COLS // 16

FLOPS = 2 * N * K * M


def tile_gather_matmul_kernel(tc, table, w, b, offs, out):
    nc = tc.nc
    with (
        tc.tile_pool(name="held", bufs=1) as held,
        tc.tile_pool(name="results", bufs=1) as results,
        tc.psum_pool(name="psum", bufs=1) as psum,
    ):
        offsets = held.tile([P, N // 16], U16)
        bias = held.tile([P, 1], F32)
        features = [held.tile([P, TOKENS], BF16, name=f"features{a}") for a in range(BLOCKS)]
        weights = [held.tile([P, EXPERTS // 2, BLOCKS, M], BF16, name=f"weights{h}") for h in range(2)]

        table_blocks = table.rearrange("(p a) s -> a p s", a=BLOCKS)
        w_blocks = w.rearrange("e (p a) m -> p e a m", a=BLOCKS)

        nc.sync.dma_start(offsets[:], offs)
        nc.sync.dma_start(features[0][:], table_blocks[0])
        nc.scalar.dma_start(weights[0][:], w_blocks[:, : EXPERTS // 2])
        nc.sync.dma_start(features[1][:], table_blocks[1])
        nc.sync.dma_start(weights[1][:], w_blocks[:, EXPERTS // 2 :])
        nc.scalar.dma_start(bias[:], b)

        sums = [psum.tile([P, COLS], F32, name=f"sums{t}") for t in range(TILES)]

        def multiply(t, a):
            expert = t // TILES_PER_EXPERT
            nc.tensor.matmul(
                sums[t][:],
                weights[expert // 2][:, expert % 2, a, :],
                features[a][:].indirect(offsets[:, t * LIST_COLS : (t + 1) * LIST_COLS]),
                start=(a == 0),
                stop=(a == BLOCKS - 1),
            )

        def finish(t):
            parts = 2 if t == TILES - 1 else 1
            width = COLS // parts
            for h in range(parts):
                result = results.tile([P, width], F32, name=f"result{t}_{h}")
                source = sums[t][:, h * width : (h + 1) * width]
                if t % 2 == 1:
                    nc.vector.tensor_scalar(result[:], source, bias[:], 0.0, ADD, MAX)
                else:
                    nc.scalar.activation(result[:], source, RELU, bias=bias[:])
                first = t * COLS + h * width
                nc.sync.dma_start(out[:, first : first + width], result[:])

        for t in range(TILES // 2):
            multiply(t, 0)
        for t in range(TILES // 2):
            multiply(t, 1)
            finish(t)
        for t in range(TILES // 2, TILES):
            for a in range(BLOCKS):
                multiply(t, a)
            finish(t)
